import numpy as np, ml_dtypes
CORES = [144,200,272,328,400,456]
N = 6
S, T = 8192, 1024
def entries(a): return a.T.reshape(-1)
def pack(v, P): return np.ascontiguousarray(np.asarray(v, np.int32).reshape(-1, P).T)
def lists(rng, how):
    M = rng.integers(0, S, (N, S)); b = rng.integers(0, S, T)
    if how == "alike": M = np.stack([rng.permutation(S) for f in range(N)]); b[:] = rng.integers(S)
    if how == "edge":
        M = np.where(rng.random((N, S)) < 0.5, 0, S - 1); w = rng.permutation(N) % 2 * (S - 1); M[:, 0] = w; M[:, S - 1] = S - 1 - w
        b = np.where(rng.random(T) < 0.5, 0, S - 1); b[rng.permutation(T)[:2]] = [0, S - 1]
    if how == "fold":
        V = np.stack([rng.permutation(S)[:4] for f in range(N + 1)]); M = V[np.arange(N)[:, None], rng.integers(0, 4, (N, S))]
        M[np.arange(N)[:, None], V[1:]] = V[:N]; b[rng.permutation(T)[:4]] = V[N]
    if how == "mixed":
        k = np.concatenate([[3, 3], rng.permutation(np.arange(N - 2) % 3)])
        for f in range(N): M[f] = [np.arange(S), rng.permutation(S), M[f], rng.integers(0, S, 4)[rng.integers(0, 4, S)]][k[f]]
    if how == "turn": M = np.stack([rng.permutation(S) for f in range(N)]); b = rng.permutation(S)[:T]
    return {"bp": np.stack([pack(m, 16) for m in M]), "st": np.broadcast_to(pack(b, 16), (N, 16, T // 16)).copy()}
def setup_inputs(rng):
    return dict({"tab": rng.standard_normal((N, 128, S), dtype=np.float32).astype(ml_dtypes.bfloat16)}, **lists(rng, "uniform"))
def setup_inputs_alike(rng):
    d = setup_inputs(rng); d.update(lists(rng, "alike"))
    for k in ("tab",): d[k] = (d[k].astype(np.float32) * 1048576.0).astype(d[k].dtype)
    return d
def setup_inputs_edge(rng):
    d = setup_inputs(rng); d.update(lists(rng, "edge"))
    for k in ("tab",): d[k] = (d[k].astype(np.float32) * (1 / 1024.0)).astype(d[k].dtype)
    return d
def setup_inputs_fold(rng):
    d = setup_inputs(rng); d.update(lists(rng, "fold"))
    return d
def setup_inputs_mixed(rng):
    d = setup_inputs(rng); d.update(lists(rng, "mixed"))
    return d
def setup_inputs_turn(rng):
    d = setup_inputs(rng); d.update(lists(rng, "turn"))
    return d
def check_inputs(x):
    bad = []
    if x["bp"].min() < 0 or x["bp"].max() >= S: bad.append("bp out of range")
    if x["st"].min() < 0 or x["st"].max() >= S: bad.append("st out of range")
    if not all(np.array_equal(a, x["st"][0]) for a in x["st"]): bad.append("st isn't alike on all ranks")
    return bad
def reference(tab, bp, st):
    b = entries(st[0]); y = np.zeros((N, 128, T), tab.dtype)
    for f in range(N - 1, -1, -1):
        y[f] = tab[f][:, b]
        b = entries(bp[f])[b]
    return {"y": y}

@@ -1,0 +1,277 @@
+from concourse.bass import DstId, RemoteDMATransfer
+from concourse.mybir import AluOpType as A, ActivationFunctionType as F
+
+S = 8192
+SCRATCH = {n: ("sbuf", [128, w], d) for d, lst in {
+    "bfloat16": [("tabs", S), ("WA", S), ("WB", S), ("WC", S), ("zt", 1024), ("D", 128), ("X", 128), ("ZL", 128), ("BD", 128),
+                 ("BP0", 8), ("BP1", 8), ("BV", 64), ("ya", 512), ("yb", 512)],
+    "float32": [("XF", 128), ("E", 128), ("R", 128), ("Z", 64), ("cr", 128), ("cg", 128), ("nlo", 64), ("nhi", 64), ("rf", 4),
+                ("gf", 4), ("w1", 16), ("nz", 4), ("eq8", 8), ("SGF", 8), ("LOF", 8), ("b4s", 8), ("b4", 8), ("t1", 8),
+                ("t2", 8), ("t3", 8)],
+    "int32": [("W16", 512), ("V2", 128), ("I2", 128), ("pi", 4), ("rg", 8), ("SG", 8), ("LO", 8), ("hq", 8)],
+    "uint16": [("off", 8), ("offy", 64)]}.items() for n, w in lst}
+SCRATCH.update({n: ("psum", [128, 512], "float32") for n in ("psA", "psF", "psG")})
+SCRATCH.update({"land%d" % k: ("dram", [128, 128], "bfloat16") for k in (1, 2, 3, 4)})
+SCRATCH["b4d"] = ("dram", [128, 8], "float32")
+SEMAPHORES = ["v", "iot", "ldb", "dr", "sent", "tabl", "zz", "zA", "zB", "zBg", "zC", "zCs", "arr1", "arr2", "arr3", "arr4",
+              "arrb", "win1", "win2", "win3", "win4", "x", "pe", "cst", "oy", "yv", "ys", "st", "lds"]
+
+
+def pick(mask, n):
+    bits = [b for b in range(16) if mask >> b & 1][:8]
+    n = min(n, len(bits))
+    return sum(1 << b for b in bits[::len(bits) // n][:n])
+
+
+def plan(T, topo):
+    c = T.cores
+
+    def ports(rank, target):
+        own = c[rank]
+        chip = [k for k in range(512) if topo.host(k) == topo.host(own) and topo.chip(k) == topo.chip(own) and k != own]
+        return sorted([k for k in chip if topo.may_write(k, c[target])], key=lambda k: (topo.die(k) != topo.die(own), k))
+
+    p4, p2 = ports(2, 1)[0], ports(2, 1)[-1]
+    p5, p3 = ports(3, 0)[0], ports(3, 0)[1]
+    p1 = ports(1, 0)[0]
+    return {
+        c[5]: [("b", [p5], 8)], p5: [("b", [c[0], c[1]], 8), ("b", [c[2], c[3], c[4]], 8)],
+        c[4]: [(4, [p4], 8)], p4: [(4, [c[0]], 4), (4, [c[1], c[3], c[2]], 4)],
+        c[3]: [(3, [p3, c[1]], 8)], p3: [(3, [c[0]], 4), (3, [c[2]], 4)],
+        c[2]: [(2, [c[0], p2], 8)], p2: [(2, [c[1]], 4)],
+        c[1]: [(1, [p1], 8)], p1: [(1, [c[0]], 4)],
+    }
+
+
+def rank_program(g, core, T, topo):
+    f = T.rank_of(core)
+    calls = plan(T, topo)
+    if core not in calls and f is None:
+        return
+    s = T.sem
+    arrive = {piece: n for lst in calls.values() for piece, dsts, n in lst if core in dsts}
+    arrsem = {k: s["arr%s" % k] for k in (1, 2, 3, 4, "b")}
+    nsent = sum(n for _, _, n in calls.get(core, []))
+
+    def send(piece, dsts, n):
+        if piece == "b":
+            src = T.b4s[:, :] if f == 5 else T.b4d[:, :]
+            dst = T.b4d[:, :] if f == 5 else T.b4[:, :]
+        else:
+            src = T.D[:, :] if f is not None else T["land%d" % piece][:, :]
+            dst = T["land%d" % piece][:, :]
+        mask = 0xFFFF
+        for d in dsts:
+            mask &= topo.mask(core, d)
+        ids = [topo.addr(d, core) for d in dsts]
+        g.remote_dma_fused([RemoteDMATransfer(dst_ids=[DstId(rid=r, pnc=p) for r, p in ids], dma_engine_mask=pick(mask, n),
+                                              remote_sem=arrsem[piece], srcs=[src], dsts=[dst] * len(dsts), alu_op=0)],
+                           local_sem=s.sent)
+
+    if f is None:
+        piece = calls[core][0][0]
+        g.wait_ge(arrsem[piece], arrive[piece])
+        for c in calls[core]:
+            send(*c)
+        g.wait_ge(s.sent, nsent)
+        return
+
+    V, Q, C, P = g.vector, g.sync, g.scalar, g.tensor
+    cnt = {"v": 0, "x": 0, "pe": 0}
+
+    def vi(ins):
+        cnt["v"] += 1
+        return ins.then_inc(s.v, 1)
+
+    def vw():
+        V.wait_ge(s.v, cnt["v"])
+
+    def xi(ins=None):
+        cnt["x"] += 1
+        if ins is None:
+            vw()
+            V.sem_inc(s.x, 1)
+        else:
+            ins.then_inc(s.x, 1)
+        P.wait_ge(s.x, cnt["x"])
+
+    def pei(ins):
+        cnt["pe"] += 1
+        ins.then_inc(s.pe, 1)
+        V.wait_ge(s.pe, cnt["pe"])
+
+    def ts(out, in0, s1, op0, s2=None, op1=None):
+        if op1 is None:
+            return V.tensor_scalar(out=out, in0=in0, scalar1=s1, scalar2=None, op0=op0)
+        return V.tensor_scalar(out=out, in0=in0, scalar1=s1, scalar2=s2, op0=op0, op1=op1)
+
+    if f == 5:
+        for k in range(8):
+            (Q, C)[k % 2].dma_start(T.SG[16 * k:16 * k + 16, :], T.st[:, 8 * k:8 * k + 8]).then_inc(s.lds, 16)
+        for k in range(8):
+            (Q, C)[k % 2].dma_start(T.W16[16 * k:16 * k + 16, :], T.bp[:, :]).then_inc(s.ldb, 16)
+    elif f >= 1:
+        Q.dma_start(T.V2[0:64, :], T.bp[:, :]).then_inc(s.ldb, 16)
+        C.dma_start(T.V2[64:128, :], T.bp[:, :]).then_inc(s.ldb, 16)
+    NT = 4
+    for k in range(NT):
+        if f > 0 and k == 1:
+            Q.wait_ge(s.sent, nsent)
+        w = S // NT
+        Q.dma_start(T.tabs[:, k * w:(k + 1) * w], T.tab[:, k * w:(k + 1) * w]).then_inc(s.tabl, 16)
+
+    iotas = [(T.cr, [[0, 8], [1, 16]]), (T.nlo, [[0, 8], [1, 8]])]
+    iotas += [(T.nhi, [[1, 8], [0, 8]])] if f <= 3 else [(T.cg, [[1, 8], [0, 16]])] if f == 5 else []
+    g.iota(T.pi[:, 0:1], [[1, 1]], 0, 1).then_inc(s.iot, 1)
+    for t, pat in iotas:
+        g.iota(t[:, :], pat, 0, 0, allow_small_or_imprecise_dtypes=True).then_inc(s.iot, 1)
+
+    maps = list(range(4, f, -1))
+    place = {0: {4: ("A", 0), 2: ("A", 1), 3: ("B", 0), 1: ("C", 0)}, 1: {4: ("A", 0), 3: ("B", 0), 2: ("C", 0)},
+             2: {4: ("A", 0), 3: ("B", 0)}, 3: {4: ("A", 0)}}.get(f, {})
+    wins = sorted({w for w, _ in place.values()})
+    if "C" in wins:
+        V.memset(T.zt[:, :], 0.0).then_inc(s.zz, 1)
+
+    def constants():
+        vi(V.memset(T.nz[:, :], -0.0))
+        V.wait_ge(s.iot, 1 + len(iotas))
+        vi(ts(T.rg[:, 0:1], T.pi[:, 0:1], 15, A.bitwise_and))
+        vi(ts(T.rg[:, 4:5], T.pi[:, 0:1], 4, A.logical_shift_right))
+        vw()
+        vi(V.tensor_copy(T.rf[:, 0:1], T.rg[:, 0:1]))
+        vi(V.tensor_copy(T.gf[:, 0:1], T.rg[:, 4:5]))
+        vw()
+        r, gg = T.rf[:, 0:1], T.gf[:, 0:1]
+        vi(ts(T.R[:, :], T.cr[:, :], r, A.is_equal))
+        vi(ts(T.eq8[:, :], T.nlo[:, 0:8], gg, A.is_equal))
+        if f == 5:
+            vi(ts(T.BD[:, :], T.cg[:, :], gg, A.is_equal))
+        if maps:
+            slots = sorted({k for _, k in place.values()})
+            last = place[maps[-1]][1]
+            for k in slots:
+                vi(ts(T.w1[:, 4 * k:4 * k + 1], r, float(2 * k), A.is_equal, 512.0, A.mult))
+                vi(ts(T.w1[:, 4 * k + 1:4 * k + 2], r, float(2 * k + 1), A.is_equal))
+            vi(ts(T.w1[:, 8:9], r, float(2 * last), A.is_equal))
+            vi(ts(T.w1[:, 9:10], r, float(2 * last + 1), A.is_equal, 16.0, A.mult))
+            vw()
+            for k in slots + [2]:
+                vi(V.tensor_tensor(T.w1[:, 4 * k + 2:4 * k + 3], T.w1[:, 4 * k:4 * k + 1], T.w1[:, 4 * k + 1:4 * k + 2], A.add))
+            vw()
+            for k in slots:
+                vi(ts(T["BP%d" % k][:, :], T.nlo[:, 0:8], gg, A.is_equal, T.w1[:, 4 * k + 2:4 * k + 3], A.mult))
+            sel, oth = (T.nlo, T.nhi) if maps[-1] % 2 == 0 else (T.nhi, T.nlo)
+            vi(ts(T.BV[:, :], sel[:, :], gg, A.is_equal, T.w1[:, 10:11], A.mult))
+            vi(ts(T.MK[:, :], oth[:, :], gg, A.is_equal)) if False else vi(ts(T.cg[:, 0:64], oth[:, :], gg, A.is_equal))
+        vw()
+        V.sem_inc(s.cst, 1)
+
+    HB, HC = 5120, 6144
+
+    def zeros():
+        if "A" in wins:
+            V.memset(T.WA[:, :], 0.0).then_inc(s.zA, 1)
+        if "B" in wins:
+            g.iota(T.WB[:, HB:], [[0, S - HB]], 0, 0, allow_small_or_imprecise_dtypes=True).then_inc(s.zBg, 1)
+            V.memset(T.WB[:, 0:HB], 0.0).then_inc(s.zB, 1)
+        if "C" in wins:
+            V.memset(T.WC[:, HC:], 0.0).then_inc(s.zC, 1)
+            C.wait_ge(s.zz, 1)
+            for k in range(0, HC, 1024):
+                C.activation(T.WC[:, k:k + 1024], T.zt[:, :], F.Copy).then_inc(s.zCs, 1)
+
+    if f == 0:
+        zeros()
+        constants()
+    else:
+        constants()
+        if f <= 4:
+            V.wait_ge(s.ldb, 32)
+            vi(ts(T.I2[0:64, :], T.V2[0:64, :], 15, A.bitwise_and))
+            vi(ts(T.I2[64:128, :], T.V2[64:128, :], 0.0625, A.mult, -256.46875, A.add))
+            vw()
+            V.tensor_copy(T.D[:, :], T.I2[:, :]).then_inc(s.dr, 1)
+            g.wait_ge(s.dr, 1)
+            send(*calls[core][0])
+        zeros()
+
+    order = {0: [2, 4, 3, 1], 1: [3, 4, 2], 2: [4, 3], 3: [4]}.get(f, [])
+    for m in order:
+        w, k = place[m]
+        for q, half in ((Q, range(0, 4)), (C, range(4, 8))):
+            q.wait_ge(arrsem[m], arrive[m])
+            for z in {"A": [("zA", 1)], "B": [("zB", 1), ("zBg", 1)], "C": [("zC", 1), ("zCs", HC // 1024)]}[w]:
+                q.wait_ge(s[z[0]], z[1])
+            for grp in half:
+                lo = 16 * grp + 2 * k
+                q.dma_start(T["W" + w][lo:lo + 2, :], T["land%d" % m][:, :]).then_inc(s["win%d" % m], 16)
+
+    if f == 5:
+        V.wait_ge(s.lds, 128)
+        vi(ts(T.LO[:, :], T.SG[:, :], 15, A.bitwise_and))
+        vi(ts(T.hq[:, :], T.SG[:, :], 4, A.logical_shift_right))
+        vw()
+        vi(V.tensor_copy(T.LOF[:, :], T.LO[:, :]))
+        vi(V.tensor_copy(T.off[:, :], T.hq[:, :]))
+        vi(V.tensor_copy(T.SGF[:, :], T.SG[:, :]))
+        vw()
+        for k in range(8):
+            vi(ts(T.ZL[:, 16 * k:16 * k + 16], T.cr[:, 0:16], T.rf[:, 0:1], A.is_equal, T.LOF[:, k:k + 1], A.mult))
+        xi()
+        pei(P.matmul(T.psA[:, 0:128], T.BD[:, :], T.ZL[:, :], True, True))
+        vi(ts(T.E[:, :], T.psA[:, 0:128], T.rf[:, 0:1], A.is_equal))
+        vw()
+        V.wait_ge(s.ldb, 128)
+        xi(V.tensor_tensor(T.XF[:, :], T.W16[:, :].indirect(T.off[:, 0:8]), T.E[:, :], A.mult))
+        pei(P.matmul(T.psF[:, 0:8], T.XF[:, :], T.eq8[:, :], True, True))
+        V.tensor_copy(T.b4s[:, :], T.psF[:, 0:8]).then_inc(s.dr, 1)
+        g.wait_ge(s.dr, 1)
+        send(*calls[core][0])
+    else:
+        V.wait_ge(arrsem["b"], arrive["b"])
+    P.wait_ge(s.cst, 1)
+    if f >= 4:
+        for k in range(8):
+            cols, src = (T.Z[:, 8 * k:8 * k + 8], T.SGF) if f == 5 else (T.Z[:, k::8], T.b4)
+            vi(ts(cols, src[:, 0:8], T.eq8[:, k:k + 1], A.mult))
+        xi()
+    else:
+        vi(ts(T.hq[:, :], T.b4[:, :], 0.0625, A.mult, -0.46875, A.add))
+        vi(ts(T.t1[:, :], T.b4[:, :], 512.0, A.mult))
+        vw()
+        vi(ts(T.t2[:, :], T.hq[:, :], -8191.0, A.mult))
+        vw()
+        vi(V.tensor_tensor(T.t3[:, :], T.t1[:, :], T.t2[:, :], A.add))
+        vw()
+        vi(V.tensor_copy(T.off[:, :], T.t3[:, :]))
+        vw()
+        for m in maps:
+            w, k = place[m]
+            for mm in order:
+                if place[mm][0] == w:
+                    V.wait_ge(s["win%d" % mm], 128)
+            xi(V.tensor_copy(T.X[:, :], T["W" + w][:, :].indirect(T.off[:, 0:8])))
+            if m != maps[-1]:
+                pei(P.matmul(T.psA[:, 0:8], T.X[:, :], T["BP%d" % k][:, :], True, True))
+                vi(ts(T.off[:, :], T.psA[:, 0:8], 256.0, A.add))
+                vw()
+            else:
+                pei(P.matmul(T.psF[:, 0:64], T.X[:, :], T.BV[:, :], True, True))
+                xi(V.tensor_tensor(T.Z[:, :], T.psF[:, 0:64], T.cg[:, 0:64], A.mult))
+    pei(P.matmul(T.psG[:, 0:64], T.R[:, :], T.Z[:, :], True, True))
+    ts(T.offy[:, :], T.psG[:, 0:64], 0.0 if f >= 4 else 4096.0, A.add).then_inc(s.oy, 1)
+
+    for q in (V, C):
+        q.wait_ge(s.oy, 1)
+        q.wait_ge(s.tabl, 16 * NT)
+    V.tensor_copy(T.ya[:, :], T.tabs[:, :].indirect(T.offy[:, 0:32])).then_inc(s.yv, 1)
+    C.wait_ge(s.cst, 1)
+    C.activation(T.yb[:, :], T.tabs[:, :].indirect(T.offy[:, 32:64]), F.Identity, bias=T.nz[:, 0:1]).then_inc(s.ys, 1)
+    Q.wait_ge(s.yv, 1)
+    Q.dma_start(T.y[:, 0:512], T.ya[:, :]).then_inc(s.st, 16)
+    C.wait_ge(s.ys, 1)
+    C.dma_start(T.y[:, 512:1024], T.yb[:, :]).then_inc(s.st, 16)
+    Q.wait_ge(s.st, 32)
+    if nsent:
+        g.wait_ge(s.sent, nsent)

@@ -7,14 +7,15 @@ SCRATCH = {n: ("sbuf", [128, w], d) for d, lst in {
                  ("BP0", 8), ("BP1", 8), ("BV", 64), ("ya", 512), ("yb", 512)],
     "float32": [("XF", 128), ("E", 128), ("R", 128), ("Z", 64), ("cr", 128), ("cg", 128), ("nlo", 64), ("nhi", 64), ("rf", 4),
                 ("gf", 4), ("w1", 16), ("nz", 4), ("eq8", 8), ("SGF", 8), ("LOF", 8), ("b4s", 8), ("b4", 8), ("t1", 8),
-                ("t2", 8), ("t3", 8)],
+                ("t2", 8), ("t3", 8), ("MK", 64)],
     "int32": [("W16", 512), ("V2", 128), ("I2", 128), ("pi", 4), ("rg", 8), ("SG", 8), ("LO", 8), ("hq", 8)],
     "uint16": [("off", 8), ("offy", 64)]}.items() for n, w in lst}
 SCRATCH.update({n: ("psum", [128, 512], "float32") for n in ("psA", "psF", "psG")})
 SCRATCH.update({"land%d" % k: ("dram", [128, 128], "bfloat16") for k in (1, 2, 3, 4)})
 SCRATCH["b4d"] = ("dram", [128, 8], "float32")
 SEMAPHORES = ["v", "iot", "ldb", "dr", "sent", "tabl", "zz", "zA", "zB", "zBg", "zC", "zCs", "arr1", "arr2", "arr3", "arr4",
-              "arrb", "win1", "win2", "win3", "win4", "x", "pe", "cst", "oy", "yv", "ys", "st", "lds"]
+              "arrb", "arrc", "win1", "win2", "win3", "win4", "x", "pe", "cst", "oy", "yv", "ys", "st", "lds", "lof", "zls"]
+TILES = {"cr": [[0, 8], [1, 16]], "cg": [[1, 8], [0, 16]], "nlo": [[0, 8], [1, 8]], "nhi": [[1, 8], [0, 8]]}
 
 
 def pick(mask, n):
@@ -35,11 +36,14 @@ def plan(T, topo):
     p5, p3 = ports(3, 0)[0], ports(3, 0)[1]
     p1 = ports(1, 0)[0]
     return {
-        c[5]: [("b", [p5], 8)], p5: [("b", [c[0], c[1]], 8), ("b", [c[2], c[3], c[4]], 8)],
-        c[4]: [(4, [p4], 8)], p4: [(4, [c[0]], 4), (4, [c[1], c[3], c[2]], 4)],
-        c[3]: [(3, [p3, c[1]], 8)], p3: [(3, [c[0]], 4), (3, [c[2]], 4)],
+        c[5]: [("nlo", [c[3]], 8), ("b", [p5], 8)],
+        p5: [("nhi", [c[0]], 8), ("b", [c[0]], 8), ("b", [c[1]], 8), ("b", [c[2], c[3], c[4]], 8)],
+        c[4]: [("nlo", [c[2]], 8), (4, [p4], 8)],
+        p4: [("nlo", [c[0]], 4), (4, [c[0]], 4), (4, [c[1]], 4), (4, [c[3], c[2]], 4)],
+        c[3]: [("nhi", [c[1]], 8), (3, [p3, c[1]], 8)],
+        p3: [("cr", [c[2]], 4), (3, [c[0]], 4), (3, [c[2]], 4)],
         c[2]: [(2, [c[0], p2], 8)], p2: [(2, [c[1]], 4)],
-        c[1]: [(1, [p1], 8)], p1: [(1, [c[0]], 4)],
+        c[1]: [("cr", [c[3]], 8), (1, [p1], 8)], p1: [("cr", [c[0]], 4), (1, [c[0]], 4)],
     }
 
 
@@ -49,12 +53,18 @@ def rank_program(g, core, T, topo):
     if core not in calls and f is None:
         return
     s = T.sem
-    arrive = {piece: n for lst in calls.values() for piece, dsts, n in lst if core in dsts}
+    mine = calls.get(core, [])
+    comes = [(piece, n) for lst in calls.values() for piece, dsts, n in lst if core in dsts]
+    arrive = dict(comes)
+    nconst = sum(n for piece, n in comes if piece in TILES)
     arrsem = {k: s["arr%s" % k] for k in (1, 2, 3, 4, "b")}
-    nsent = sum(n for _, _, n in calls.get(core, []))
+    nsent = sum(n for _, _, n in mine)
+    niota = [0]
 
     def send(piece, dsts, n):
-        if piece == "b":
+        if piece in TILES:
+            src = dst = T[piece][:, :]
+        elif piece == "b":
             src = T.b4s[:, :] if f == 5 else T.b4d[:, :]
             dst = T.b4d[:, :] if f == 5 else T.b4[:, :]
         else:
@@ -65,13 +75,20 @@ def rank_program(g, core, T, topo):
             mask &= topo.mask(core, d)
         ids = [topo.addr(d, core) for d in dsts]
         g.remote_dma_fused([RemoteDMATransfer(dst_ids=[DstId(rid=r, pnc=p) for r, p in ids], dma_engine_mask=pick(mask, n),
-                                              remote_sem=arrsem[piece], srcs=[src], dsts=[dst] * len(dsts), alu_op=0)],
-                           local_sem=s.sent)
+                                              remote_sem=s.arrc if piece in TILES else arrsem[piece],
+                                              srcs=[src], dsts=[dst] * len(dsts), alu_op=0)], local_sem=s.sent)
+
+    def iota(name):
+        g.iota(T[name][:, :], TILES[name], 0, 0, allow_small_or_imprecise_dtypes=True).then_inc(s.iot, 1)
+        niota[0] += 1
 
     if f is None:
-        piece = calls[core][0][0]
-        g.wait_ge(arrsem[piece], arrive[piece])
-        for c in calls[core]:
+        for k, c in enumerate(mine):
+            if c[0] in TILES:
+                iota(c[0])
+                g.wait_ge(s.iot, 1)
+            elif k == 0 or mine[k - 1][0] in TILES:
+                g.wait_ge(arrsem[c[0]], arrive[c[0]])
             send(*c)
         g.wait_ge(s.sent, nsent)
         return
@@ -120,11 +137,24 @@ def rank_program(g, core, T, topo):
         w = S // NT
         Q.dma_start(T.tabs[:, k * w:(k + 1) * w], T.tab[:, k * w:(k + 1) * w]).then_inc(s.tabl, 16)
 
-    iotas = [(T.cr, [[0, 8], [1, 16]]), (T.nlo, [[0, 8], [1, 8]])]
-    iotas += [(T.nhi, [[1, 8], [0, 8]])] if f <= 3 else [(T.cg, [[1, 8], [0, 16]])] if f == 5 else []
-    g.iota(T.pi[:, 0:1], [[1, 1]], 0, 1).then_inc(s.iot, 1)
-    for t, pat in iotas:
-        g.iota(t[:, :], pat, 0, 0, allow_small_or_imprecise_dtypes=True).then_inc(s.iot, 1)
+    need = [n for n in ["cr", "nlo"] + (["nhi"] if f <= 3 else ["cg"] if f == 5 else []) if n not in arrive]
+    ahead = [c for c in mine if c[0] in TILES]
+    first = [c[0] for c in ahead] if f != 5 else need
+    for n in first:
+        iota(n)
+    if f == 5:
+        g.iota(T.pi[:, 0:1], [[1, 1]], 0, 1).then_inc(s.iot, 1)
+        niota[0] += 1
+    for c in ahead:
+        g.wait_ge(s.iot, niota[0])
+        send(*c)
+    for n in need:
+        if n not in first:
+            iota(n)
+    if f != 5:
+        g.iota(T.pi[:, 0:1], [[1, 1]], 0, 1).then_inc(s.iot, 1)
+        niota[0] += 1
+    sends = [c for c in mine if c[0] not in TILES]
 
     maps = list(range(4, f, -1))
     place = {0: {4: ("A", 0), 2: ("A", 1), 3: ("B", 0), 1: ("C", 0)}, 1: {4: ("A", 0), 3: ("B", 0), 2: ("C", 0)},
@@ -135,7 +165,9 @@ def rank_program(g, core, T, topo):
 
     def constants():
         vi(V.memset(T.nz[:, :], -0.0))
-        V.wait_ge(s.iot, 1 + len(iotas))
+        V.wait_ge(s.iot, niota[0])
+        if nconst:
+            V.wait_ge(s.arrc, nconst)
         vi(ts(T.rg[:, 0:1], T.pi[:, 0:1], 15, A.bitwise_and))
         vi(ts(T.rg[:, 4:5], T.pi[:, 0:1], 4, A.logical_shift_right))
         vw()
@@ -144,7 +176,8 @@ def rank_program(g, core, T, topo):
         vw()
         r, gg = T.rf[:, 0:1], T.gf[:, 0:1]
         vi(ts(T.R[:, :], T.cr[:, :], r, A.is_equal))
-        vi(ts(T.eq8[:, :], T.nlo[:, 0:8], gg, A.is_equal))
+        if f >= 4:
+            vi(ts(T.eq8[:, :], T.nlo[:, 0:8], gg, A.is_equal))
         if f == 5:
             vi(ts(T.BD[:, :], T.cg[:, :], gg, A.is_equal))
         if maps:
@@ -163,15 +196,18 @@ def rank_program(g, core, T, topo):
                 vi(ts(T["BP%d" % k][:, :], T.nlo[:, 0:8], gg, A.is_equal, T.w1[:, 4 * k + 2:4 * k + 3], A.mult))
             sel, oth = (T.nlo, T.nhi) if maps[-1] % 2 == 0 else (T.nhi, T.nlo)
             vi(ts(T.BV[:, :], sel[:, :], gg, A.is_equal, T.w1[:, 10:11], A.mult))
-            vi(ts(T.MK[:, :], oth[:, :], gg, A.is_equal)) if False else vi(ts(T.cg[:, 0:64], oth[:, :], gg, A.is_equal))
+            vi(ts(T.MK[:, :], oth[:, :], gg, A.is_equal))
         vw()
         V.sem_inc(s.cst, 1)
 
     HB, HC = 5120, 6144
 
-    def zeros():
+    def zero_a(half):
         if "A" in wins:
-            V.memset(T.WA[:, :], 0.0).then_inc(s.zA, 1)
+            V.memset(T.WA[:, half * 4096:half * 4096 + 4096], 0.0).then_inc(s.zA, 1)
+
+    def zeros():
+        zero_a(1)
         if "B" in wins:
             g.iota(T.WB[:, HB:], [[0, S - HB]], 0, 0, allow_small_or_imprecise_dtypes=True).then_inc(s.zBg, 1)
             V.memset(T.WB[:, 0:HB], 0.0).then_inc(s.zB, 1)
@@ -181,44 +217,45 @@ def rank_program(g, core, T, topo):
             for k in range(0, HC, 1024):
                 C.activation(T.WC[:, k:k + 1024], T.zt[:, :], F.Copy).then_inc(s.zCs, 1)
 
-    if f == 0:
-        zeros()
-        constants()
-    else:
-        constants()
-        if f <= 4:
-            V.wait_ge(s.ldb, 32)
-            vi(ts(T.I2[0:64, :], T.V2[0:64, :], 15, A.bitwise_and))
-            vi(ts(T.I2[64:128, :], T.V2[64:128, :], 0.0625, A.mult, -256.46875, A.add))
-            vw()
-            V.tensor_copy(T.D[:, :], T.I2[:, :]).then_inc(s.dr, 1)
-            g.wait_ge(s.dr, 1)
-            send(*calls[core][0])
-        zeros()
+    zero_a(0)
+    if 1 <= f <= 4:
+        V.wait_ge(s.ldb, 32)
+        vi(ts(T.I2[0:64, :], T.V2[0:64, :], 15, A.bitwise_and))
+        vi(ts(T.I2[64:128, :], T.V2[64:128, :], 0.0625, A.mult, -256.46875, A.add))
+        vw()
+        V.tensor_copy(T.D[:, :], T.I2[:, :]).then_inc(s.dr, 1)
+        g.wait_ge(s.dr, 1)
+        send(*sends[0])
+    zeros()
+    constants()
 
     order = {0: [2, 4, 3, 1], 1: [3, 4, 2], 2: [4, 3], 3: [4]}.get(f, [])
     for m in order:
         w, k = place[m]
         for q, half in ((Q, range(0, 4)), (C, range(4, 8))):
             q.wait_ge(arrsem[m], arrive[m])
-            for z in {"A": [("zA", 1)], "B": [("zB", 1), ("zBg", 1)], "C": [("zC", 1), ("zCs", HC // 1024)]}[w]:
+            for z in {"A": [("zA", 2)], "B": [("zB", 1), ("zBg", 1)], "C": [("zC", 1), ("zCs", HC // 1024)]}[w]:
                 q.wait_ge(s[z[0]], z[1])
             for grp in half:
                 lo = 16 * grp + 2 * k
                 q.dma_start(T["W" + w][lo:lo + 2, :], T["land%d" % m][:, :]).then_inc(s["win%d" % m], 16)
 
+    P.wait_ge(s.cst, 1)
     if f == 5:
         V.wait_ge(s.lds, 128)
         vi(ts(T.LO[:, :], T.SG[:, :], 15, A.bitwise_and))
         vi(ts(T.hq[:, :], T.SG[:, :], 4, A.logical_shift_right))
         vw()
-        vi(V.tensor_copy(T.LOF[:, :], T.LO[:, :]))
-        vi(V.tensor_copy(T.off[:, :], T.hq[:, :]))
-        vi(V.tensor_copy(T.SGF[:, :], T.SG[:, :]))
-        vw()
-        for k in range(8):
-            vi(ts(T.ZL[:, 16 * k:16 * k + 16], T.cr[:, 0:16], T.rf[:, 0:1], A.is_equal, T.LOF[:, k:k + 1], A.mult))
+        V.tensor_copy(T.LOF[:, :], T.LO[:, :]).then_inc(s.lof, 1)
+        C.wait_ge(s.cst, 1)
+        for q in (V, C):
+            q.wait_ge(s.lof, 1)
+        for k in range(4):
+            vi(ts(T.ZL[:, 16 * k:16 * k + 16], T.R[:, 0:16], T.LOF[:, k:k + 1], A.mult))
+            C.activation(T.ZL[:, 16 * k + 64:16 * k + 80], T.R[:, 0:16], F.Copy, scale=T.LOF[:, k + 4:k + 5]).then_inc(s.zls, 1)
         xi()
+        P.wait_ge(s.zls, 4)
+        vi(V.tensor_copy(T.off[:, :], T.hq[:, :]))
         pei(P.matmul(T.psA[:, 0:128], T.BD[:, :], T.ZL[:, :], True, True))
         vi(ts(T.E[:, :], T.psA[:, 0:128], T.rf[:, 0:1], A.is_equal))
         vw()
@@ -227,10 +264,11 @@ def rank_program(g, core, T, topo):
         pei(P.matmul(T.psF[:, 0:8], T.XF[:, :], T.eq8[:, :], True, True))
         V.tensor_copy(T.b4s[:, :], T.psF[:, 0:8]).then_inc(s.dr, 1)
         g.wait_ge(s.dr, 1)
-        send(*calls[core][0])
+        send(*sends[0])
+        vi(V.tensor_copy(T.SGF[:, :], T.SG[:, :]))
+        vw()
     else:
         V.wait_ge(arrsem["b"], arrive["b"])
-    P.wait_ge(s.cst, 1)
     if f >= 4:
         for k in range(8):
             cols, src = (T.Z[:, 8 * k:8 * k + 8], T.SGF) if f == 5 else (T.Z[:, k::8], T.b4)
@@ -258,7 +296,7 @@ def rank_program(g, core, T, topo):
                 vw()
             else:
                 pei(P.matmul(T.psF[:, 0:64], T.X[:, :], T.BV[:, :], True, True))
-                xi(V.tensor_tensor(T.Z[:, :], T.psF[:, 0:64], T.cg[:, 0:64], A.mult))
+                xi(V.tensor_tensor(T.Z[:, :], T.psF[:, 0:64], T.MK[:, :], A.mult))
     pei(P.matmul(T.psG[:, 0:64], T.R[:, :], T.Z[:, :], True, True))
     ts(T.offy[:, :], T.psG[:, 0:64], 0.0 if f >= 4 else 4096.0, A.add).then_inc(s.oy, 1)
 

@@ -3,19 +3,30 @@ from concourse.mybir import AluOpType as A, ActivationFunctionType as F
 
 S = 8192
 SCRATCH = {n: ("sbuf", [128, w], d) for d, lst in {
-    "bfloat16": [("tabs", S), ("WA", S), ("WB", S), ("WC", S), ("zt", 1024), ("D", 128), ("X", 128), ("ZL", 128), ("BD", 128),
-                 ("BP0", 8), ("BP1", 8), ("BV", 64), ("ya", 512), ("yb", 512)],
-    "float32": [("XF", 128), ("E", 128), ("R", 128), ("Z", 64), ("cr", 128), ("cg", 128), ("nlo", 64), ("nhi", 64), ("rf", 4),
-                ("gf", 4), ("w1", 16), ("nz", 4), ("eq8", 8), ("SGF", 8), ("LOF", 8), ("b4s", 8), ("b4", 8), ("t1", 8),
-                ("t2", 8), ("t3", 8), ("MK", 64)],
-    "int32": [("W16", 512), ("V2", 128), ("I2", 128), ("pi", 4), ("rg", 8), ("SG", 8), ("LO", 8), ("hq", 8)],
-    "uint16": [("off", 8), ("offy", 64)]}.items() for n, w in lst}
-SCRATCH.update({n: ("psum", [128, 512], "float32") for n in ("psA", "psF", "psG")})
+    "bfloat16": [("tabs", S), ("WA", S), ("WB", S), ("WC", S), ("zt", 1024), ("D", 128), ("X", 128), ("LOB", 128), ("BDb", 128),
+                 ("BDo", 128), ("BP0", 8), ("BP1", 8), ("L0", 128), ("L1", 128), ("t0", 128), ("t1", 128), ("tx", 128), ("n8", 8),
+                 ("lin", 64), ("ya", 512), ("yb", 512)],
+    "float32": [("XFb", 128), ("Eb", 128), ("XFo", 128), ("Eo", 128), ("TF", 128), ("L4", 128), ("R4", 64), ("cg", 128),
+                ("I16", 16), ("rf", 4), ("gf", 4), ("w1", 16), ("nz", 4), ("eq8", 8), ("b4b", 8), ("b4o", 8), ("b4", 8), ("u1", 8),
+                ("u2", 8), ("u3", 8)],
+    "int32": [("W16", 512), ("V2", 128), ("I2", 128), ("pi", 4), ("rg", 8), ("TT", 128), ("LO", 128), ("hq", 16), ("SG", 64)],
+    "uint16": [("off", 16), ("offy", 64)]}.items() for n, w in lst}
+SCRATCH.update({n: ("psum", [128, 512], "float32") for n in ("psA", "psB", "psF", "psG", "psO")})
 SCRATCH.update({"land%d" % k: ("dram", [128, 128], "bfloat16") for k in (1, 2, 3, 4)})
 SCRATCH["b4d"] = ("dram", [128, 8], "float32")
-SEMAPHORES = ["v", "iot", "ldb", "dr", "sent", "tabl", "zz", "zA", "zB", "zBg", "zC", "zCs", "arr1", "arr2", "arr3", "arr4",
-              "arrb", "arrc", "win1", "win2", "win3", "win4", "x", "pe", "cst", "oy", "yv", "ys", "st", "lds", "lof", "zls"]
-TILES = {"cr": [[0, 8], [1, 16]], "cg": [[1, 8], [0, 16]], "nlo": [[0, 8], [1, 8]], "nhi": [[1, 8], [0, 8]]}
+SEMAPHORES = ["v", "iot", "ipi", "ldb", "dr", "do", "sent", "tabl", "zz", "zA", "zB", "zC", "zAs", "zBs", "zCs", "zAg", "zBg",
+              "zCg", "trg", "arr1", "arr2", "arr3", "arr4", "arrb", "arrc", "win1", "win2", "win3", "win4", "x", "pe", "po", "pa",
+              "pb", "cst", "oy", "yv", "ys", "st", "lds", "lsg", "l4"]
+TILES = {"t0": ([[0, 8], [1, 16]], 0), "t1": ([[0, 8], [1, 16]], -1), "n8": ([[1, 8]], 0), "lin": ([[1, 64]], 0),
+         "I16": ([[1, 16]], 0), "cg": ([[1, 8], [0, 16]], 0)}
+LOAD = {0: [(8192, "")], 1: [(3072, ""), (3072, "t"), (2048, "w")], 2: [(3072, ""), (3072, "t"), (2048, "w")],
+        3: [(2048, ""), (2048, "t"), (4096, "s")], 4: [(2048, ""), (6144, "s")], 5: [(3072, ""), (5120, "s")]}
+ORDER = {0: [2, 4, 3, 1], 1: [3, 2, 4], 2: [4, 3], 3: [4]}
+FILLS = {0: [("V", "A", 0, S), ("V", "B", 0, 4096), ("g", "B", 4096, S), ("C", "C", 0, S)],
+         1: [("V", "A", 0, 1024), ("V", "A", 1024, S), ("V", "B", 0, 1024), ("C", "B", 1024, 6144), ("t", "B", 6144, 6400),
+             ("g", "B", 6400, S)],
+         3: [("V", "A", 0, 1024), ("V", "A", 1024, 4096), ("C", "A", 4096, 7168), ("t", "A", 7168, 7424), ("g", "A", 7424, S)]}
+FILLS[2] = FILLS[1]
 
 
 def pick(mask, n):
@@ -27,23 +38,27 @@ def pick(mask, n):
 def plan(T, topo):
     c = T.cores
 
-    def ports(rank, target):
+    def chip(rank):
         own = c[rank]
-        chip = [k for k in range(512) if topo.host(k) == topo.host(own) and topo.chip(k) == topo.chip(own) and k != own]
-        return sorted([k for k in chip if topo.may_write(k, c[target])], key=lambda k: (topo.die(k) != topo.die(own), k))
+        return [k for k in range(512) if topo.host(k) == topo.host(own) and topo.chip(k) == topo.chip(own) and k != own]
+
+    def ports(rank, target):
+        return sorted([k for k in chip(rank) if topo.may_write(k, c[target])], key=lambda k: (topo.die(k) != topo.die(c[rank]), k))
 
     p4, p2 = ports(2, 1)[0], ports(2, 1)[-1]
     p5, p3 = ports(3, 0)[0], ports(3, 0)[1]
     p1 = ports(1, 0)[0]
+    p6 = [k for k in chip(3) if k not in ports(3, 0) and topo.may_write(k, c[1]) and topo.die(k) == topo.die(c[3])][0]
     return {
-        c[5]: [("nlo", [c[3]], 8), ("b", [p5], 8)],
-        p5: [("nhi", [c[0]], 8), ("b", [c[0]], 8), ("b", [c[1]], 8), ("b", [c[2], c[3], c[4]], 8)],
-        c[4]: [("nlo", [c[2]], 8), (4, [p4], 8)],
-        p4: [("nlo", [c[0]], 4), (4, [c[0]], 4), (4, [c[1]], 4), (4, [c[3], c[2]], 4)],
-        c[3]: [("nhi", [c[1]], 8), (3, [p3, c[1]], 8)],
-        p3: [("cr", [c[2]], 4), (3, [c[0]], 4), (3, [c[2]], 4)],
-        c[2]: [(2, [c[0], p2], 8)], p2: [(2, [c[1]], 4)],
-        c[1]: [("cr", [c[3]], 8), (1, [p1], 8)], p1: [("cr", [c[0]], 4), (1, [c[0]], 4)],
+        c[5]: [("t1", [c[3]], 8), ("b", [p5], 8), ("o", [p6], 8)],
+        p5: [("t1", [c[0]], 8), ("b", [c[0]], 8), ("b", [c[2]], 8), ("b", [c[4]], 8)],
+        p6: [("n8", [c[1]], 8), ("o", [c[1]], 8), ("o", [c[3]], 8)],
+        c[4]: [("t0", [c[2]], 8), (4, [p4, c[2]], 8)],
+        p4: [("t0", [c[0]], 8), (4, [c[0]], 8), (4, [c[1]], 8), (4, [c[3]], 8)],
+        c[3]: [("t0", [c[1]], 8), (3, [p3, c[1]], 8)],
+        p3: [("t1", [c[2]], 4), (3, [c[0]], 4), (3, [c[2]], 4)],
+        c[2]: [("lin", [c[4]], 8), (2, [p2, c[0]], 8)], p2: [("t1", [c[1]], 4), (2, [c[1]], 4)],
+        c[1]: [("t0", [c[3]], 8), (1, [p1], 8)], p1: [("n8", [c[0]], 4), (1, [c[0]], 4)],
     }
 
 
@@ -57,15 +72,21 @@ def rank_program(g, core, T, topo):
     comes = [(piece, n) for lst in calls.values() for piece, dsts, n in lst if core in dsts]
     arrive = dict(comes)
     nconst = sum(n for piece, n in comes if piece in TILES)
-    arrsem = {k: s["arr%s" % k] for k in (1, 2, 3, 4, "b")}
+    arrsem = {1: s.arr1, 2: s.arr2, 3: s.arr3, 4: s.arr4, "b": s.arrb, "o": s.arrb}
     nsent = sum(n for _, _, n in mine)
     niota = [0]
 
+    def width(name):
+        n = 1
+        for _, k in TILES[name][0]:
+            n *= k
+        return n
+
     def send(piece, dsts, n):
         if piece in TILES:
-            src = dst = T[piece][:, :]
-        elif piece == "b":
-            src = T.b4s[:, :] if f == 5 else T.b4d[:, :]
+            src, dst = T.tx[:, 0:width(piece)], T[piece][:, :]
+        elif piece in ("b", "o"):
+            src = T["b4" + piece][:, :] if f == 5 else T.b4d[:, :]
             dst = T.b4d[:, :] if f == 5 else T.b4[:, :]
         else:
             src = T.D[:, :] if f is not None else T["land%d" % piece][:, :]
@@ -78,14 +99,15 @@ def rank_program(g, core, T, topo):
                                               remote_sem=s.arrc if piece in TILES else arrsem[piece],
                                               srcs=[src], dsts=[dst] * len(dsts), alu_op=0)], local_sem=s.sent)
 
-    def iota(name):
-        g.iota(T[name][:, :], TILES[name], 0, 0, allow_small_or_imprecise_dtypes=True).then_inc(s.iot, 1)
+    def iota(name, out):
+        pattern, base = TILES[name]
+        g.iota(out, pattern, base, 0, allow_small_or_imprecise_dtypes=True).then_inc(s.iot, 1)
         niota[0] += 1
 
     if f is None:
         for k, c in enumerate(mine):
             if c[0] in TILES:
-                iota(c[0])
+                iota(c[0], T.tx[:, 0:width(c[0])])
                 g.wait_ge(s.iot, 1)
             elif k == 0 or mine[k - 1][0] in TILES:
                 g.wait_ge(arrsem[c[0]], arrive[c[0]])
@@ -123,101 +145,119 @@ def rank_program(g, core, T, topo):
         return V.tensor_scalar(out=out, in0=in0, scalar1=s1, scalar2=s2, op0=op0, op1=op1)
 
     if f == 5:
+        Q.dma_start(T.TT[8:16, :], T.st[:, :]).then_inc(s.lds, 16)
+        for c in range(8):
+            (C, Q)[c % 2].dma_start(T.TT[c:c + 1, :], T.st[c // 4::2, 16 * (c % 4):16 * (c % 4) + 16]).then_inc(s.lds, 16)
         for k in range(8):
-            (Q, C)[k % 2].dma_start(T.SG[16 * k:16 * k + 16, :], T.st[:, 8 * k:8 * k + 8]).then_inc(s.lds, 16)
+            (C, Q)[k % 2].dma_start(T.W16[16 * k:16 * k + 16, :], T.bp[:, :]).then_inc(s.ldb, 16)
         for k in range(8):
-            (Q, C)[k % 2].dma_start(T.W16[16 * k:16 * k + 16, :], T.bp[:, :]).then_inc(s.ldb, 16)
+            C.dma_start(T.SG[16 * k:16 * k + 16, :], T.st[:, :]).then_inc(s.lsg, 16)
     elif f >= 1:
         Q.dma_start(T.V2[0:64, :], T.bp[:, :]).then_inc(s.ldb, 16)
         C.dma_start(T.V2[64:128, :], T.bp[:, :]).then_inc(s.ldb, 16)
-    NT = 4
-    for k in range(NT):
-        if f > 0 and k == 1:
-            Q.wait_ge(s.sent, nsent)
-        w = S // NT
-        Q.dma_start(T.tabs[:, k * w:(k + 1) * w], T.tab[:, k * w:(k + 1) * w]).then_inc(s.tabl, 16)
+    at = [0]
 
-    need = [n for n in ["cr", "nlo"] + (["nhi"] if f <= 3 else ["cg"] if f == 5 else []) if n not in arrive]
+    def table(when):
+        for w, t in LOAD[f]:
+            if t == when:
+                if t == "t":
+                    Q.wait_ge(s.trg, 1)
+                if t == "s":
+                    Q.wait_ge(s.sent, nsent)
+                Q.dma_start(T.tabs[:, at[0]:at[0] + w], T.tab[:, at[0]:at[0] + w]).then_inc(s.tabl, 16)
+                at[0] += w
+
+    for when in ("", "t", "s"):
+        table(when)
+
+    g.iota(T.pi[:, 0:1], [[1, 1]], 0, 1).then_inc(s.ipi, 1)
+    need = [n for n in {3: ["t0", "t1"], 4: ["lin"], 5: ["n8", "I16", "cg"]}.get(f, ["t0", "t1", "n8"]) if n not in arrive]
     ahead = [c for c in mine if c[0] in TILES]
-    first = [c[0] for c in ahead] if f != 5 else need
-    for n in first:
-        iota(n)
     if f == 5:
-        g.iota(T.pi[:, 0:1], [[1, 1]], 0, 1).then_inc(s.iot, 1)
-        niota[0] += 1
+        for n in need:
+            iota(n, T[n][:, :])
     for c in ahead:
+        iota(c[0], T.tx[:, 0:width(c[0])])
         g.wait_ge(s.iot, niota[0])
         send(*c)
-    for n in need:
-        if n not in first:
-            iota(n)
     if f != 5:
-        g.iota(T.pi[:, 0:1], [[1, 1]], 0, 1).then_inc(s.iot, 1)
-        niota[0] += 1
+        for n in need:
+            iota(n, T[n][:, :])
     sends = [c for c in mine if c[0] not in TILES]
 
     maps = list(range(4, f, -1))
-    place = {0: {4: ("A", 0), 2: ("A", 1), 3: ("B", 0), 1: ("C", 0)}, 1: {4: ("A", 0), 3: ("B", 0), 2: ("C", 0)},
+    place = {0: {4: ("A", 0), 2: ("A", 1), 3: ("B", 0), 1: ("C", 0)}, 1: {4: ("A", 1), 2: ("A", 0), 3: ("B", 0)},
              2: {4: ("A", 0), 3: ("B", 0)}, 3: {4: ("A", 0)}}.get(f, {})
-    wins = sorted({w for w, _ in place.values()})
-    if "C" in wins:
-        V.memset(T.zt[:, :], 0.0).then_inc(s.zz, 1)
 
-    def constants():
-        vi(V.memset(T.nz[:, :], -0.0))
-        V.wait_ge(s.iot, niota[0])
-        if nconst:
-            V.wait_ge(s.arrc, nconst)
-        vi(ts(T.rg[:, 0:1], T.pi[:, 0:1], 15, A.bitwise_and))
+    def numbers():
+        V.wait_ge(s.ipi, 1)
+        vi(ts(T.rg[:, 0:1], T.pi[:, 0:1], 63 if f == 4 else 15, A.bitwise_and))
         vi(ts(T.rg[:, 4:5], T.pi[:, 0:1], 4, A.logical_shift_right))
         vw()
         vi(V.tensor_copy(T.rf[:, 0:1], T.rg[:, 0:1]))
         vi(V.tensor_copy(T.gf[:, 0:1], T.rg[:, 4:5]))
-        vw()
-        r, gg = T.rf[:, 0:1], T.gf[:, 0:1]
-        vi(ts(T.R[:, :], T.cr[:, :], r, A.is_equal))
-        if f >= 4:
-            vi(ts(T.eq8[:, :], T.nlo[:, 0:8], gg, A.is_equal))
         if f == 5:
-            vi(ts(T.BD[:, :], T.cg[:, :], gg, A.is_equal))
-        if maps:
-            slots = sorted({k for _, k in place.values()})
-            last = place[maps[-1]][1]
+            vi(V.tensor_copy(T.gf[:, 2:3], T.pi[:, 0:1]))
+            vi(ts(T.gf[:, 3:4], T.pi[:, 0:1], -8.0, A.add))
+        else:
+            vi(ts(T.gf[:, 1:2], T.rg[:, 4:5], 2.0, A.mult))
+        vi(V.memset(T.nz[:, :], -0.0))
+
+    def constants():
+        vw()
+        V.wait_ge(s.iot, niota[0])
+        if nconst:
+            V.wait_ge(s.arrc, nconst)
+        r, gg = T.rf[:, 0:1], T.gf[:, 0:1]
+        if f == 5:
+            vi(ts(T.BDb[0:16, :], T.cg[0:16, :], T.gf[0:16, 3:4], A.is_equal))
+            vi(ts(T.BDo[0:16, :], T.cg[0:16, :], T.gf[0:16, 2:3], A.is_equal))
+            vi(ts(T.eq8[:, :], T.n8[:, :], gg, A.is_equal))
+            vi(ts(T.I16[0:16, :], T.I16[0:16, :], T.gf[0:16, 2:3], A.is_equal))
+        elif f == 4:
+            vi(ts(T.R4[:, :], T.lin[:, :], r, A.is_equal))
+            vi(V.memset(T.L4[:, :], 0.0))
+        else:
+            slots = sorted({place[m][1] for m in maps[:-1]})
             for k in slots:
                 vi(ts(T.w1[:, 4 * k:4 * k + 1], r, float(2 * k), A.is_equal, 512.0, A.mult))
                 vi(ts(T.w1[:, 4 * k + 1:4 * k + 2], r, float(2 * k + 1), A.is_equal))
-            vi(ts(T.w1[:, 8:9], r, float(2 * last), A.is_equal))
-            vi(ts(T.w1[:, 9:10], r, float(2 * last + 1), A.is_equal, 16.0, A.mult))
+            vi(ts(T.w1[:, 8:9], r, 0.0, A.is_equal))
+            vi(ts(T.w1[:, 9:10], r, 1.0, A.is_equal, 16.0, A.mult))
             vw()
             for k in slots + [2]:
                 vi(V.tensor_tensor(T.w1[:, 4 * k + 2:4 * k + 3], T.w1[:, 4 * k:4 * k + 1], T.w1[:, 4 * k + 1:4 * k + 2], A.add))
             vw()
             for k in slots:
-                vi(ts(T["BP%d" % k][:, :], T.nlo[:, 0:8], gg, A.is_equal, T.w1[:, 4 * k + 2:4 * k + 3], A.mult))
-            sel, oth = (T.nlo, T.nhi) if maps[-1] % 2 == 0 else (T.nhi, T.nlo)
-            vi(ts(T.BV[:, :], sel[:, :], gg, A.is_equal, T.w1[:, 10:11], A.mult))
-            vi(ts(T.MK[:, :], oth[:, :], gg, A.is_equal))
+                vi(ts(T["BP%d" % k][:, :], T.n8[:, :], gg, A.is_equal, T.w1[:, 4 * k + 2:4 * k + 3], A.mult))
+            for e in (0, 1):
+                vi(ts(T["L%d" % e][:, :], T["t%d" % e][:, :], T.gf[:, 1:2], A.is_equal, T.w1[:, 10:11], A.mult))
         vw()
         V.sem_inc(s.cst, 1)
 
-    HB, HC = 5120, 6144
+    fills = FILLS.get(f, [])
+    zeroed = {"A": {}, "B": {}, "C": {}}
 
-    def zero_a(half):
-        if "A" in wins:
-            V.memset(T.WA[:, half * 4096:half * 4096 + 4096], 0.0).then_inc(s.zA, 1)
+    def fill(k, w, lo, hi):
+        step = 1024 if k == "C" else hi - lo
+        for a in range(lo, hi, step):
+            out = T["W" + w][:, a:a + step]
+            if k == "V":
+                sem, ins = "z" + w, V.memset(out, 0.0)
+            elif k == "C":
+                sem, ins = "z" + w + "s", C.activation(out, T.zt[:, :], F.Copy)
+            else:
+                sem = "trg" if k == "t" else "z" + w + "g"
+                ins = g.iota(out, [[0, step]], 0, 0, allow_small_or_imprecise_dtypes=True)
+            ins.then_inc(s[sem], 1)
+            zeroed[w][sem] = zeroed[w].get(sem, 0) + 1
 
-    def zeros():
-        zero_a(1)
-        if "B" in wins:
-            g.iota(T.WB[:, HB:], [[0, S - HB]], 0, 0, allow_small_or_imprecise_dtypes=True).then_inc(s.zBg, 1)
-            V.memset(T.WB[:, 0:HB], 0.0).then_inc(s.zB, 1)
-        if "C" in wins:
-            V.memset(T.WC[:, HC:], 0.0).then_inc(s.zC, 1)
-            C.wait_ge(s.zz, 1)
-            for k in range(0, HC, 1024):
-                C.activation(T.WC[:, k:k + 1024], T.zt[:, :], F.Copy).then_inc(s.zCs, 1)
-
-    zero_a(0)
+    if fills:
+        V.memset(T.zt[:, :], 0.0).then_inc(s.zz, 1)
+        C.wait_ge(s.zz, 1)
+    numbers()
+    for z in fills[:1]:
+        fill(*z)
     if 1 <= f <= 4:
         V.wait_ge(s.ldb, 32)
         vi(ts(T.I2[0:64, :], T.V2[0:64, :], 15, A.bitwise_and))
@@ -226,83 +266,94 @@ def rank_program(g, core, T, topo):
         V.tensor_copy(T.D[:, :], T.I2[:, :]).then_inc(s.dr, 1)
         g.wait_ge(s.dr, 1)
         send(*sends[0])
-    zeros()
+    for z in fills[1:]:
+        fill(*z)
     constants()
 
-    order = {0: [2, 4, 3, 1], 1: [3, 4, 2], 2: [4, 3], 3: [4]}.get(f, [])
-    for m in order:
+    for m in ORDER.get(f, []):
         w, k = place[m]
-        for q, half in ((Q, range(0, 4)), (C, range(4, 8))):
+        for q, half in ((Q, range(0, 4)), (C, range(4, 8))) if f else ((Q, range(8)),):
             q.wait_ge(arrsem[m], arrive[m])
-            for z in {"A": [("zA", 2)], "B": [("zB", 1), ("zBg", 1)], "C": [("zC", 1), ("zCs", HC // 1024)]}[w]:
+            for z in zeroed[w].items():
                 q.wait_ge(s[z[0]], z[1])
             for grp in half:
                 lo = 16 * grp + 2 * k
                 q.dma_start(T["W" + w][lo:lo + 2, :], T["land%d" % m][:, :]).then_inc(s["win%d" % m], 16)
+    table("w")
 
     P.wait_ge(s.cst, 1)
     if f == 5:
-        V.wait_ge(s.lds, 128)
-        vi(ts(T.LO[:, :], T.SG[:, :], 15, A.bitwise_and))
-        vi(ts(T.hq[:, :], T.SG[:, :], 4, A.logical_shift_right))
+        V.wait_ge(s.lds, 144)
+        xi(V.tensor_copy(T.TF[0:16, :], T.TT[0:16, :]))
+        P.matmul(T.psO[:, 0:16], T.TF[0:16, :], T.I16[0:16, :], True, True).then_inc(s.po, 1)
+        vi(ts(T.LO[0:16, :], T.TT[0:16, :], 15, A.bitwise_and))
         vw()
-        V.tensor_copy(T.LOF[:, :], T.LO[:, :]).then_inc(s.lof, 1)
-        C.wait_ge(s.cst, 1)
-        for q in (V, C):
-            q.wait_ge(s.lof, 1)
-        for k in range(4):
-            vi(ts(T.ZL[:, 16 * k:16 * k + 16], T.R[:, 0:16], T.LOF[:, k:k + 1], A.mult))
-            C.activation(T.ZL[:, 16 * k + 64:16 * k + 80], T.R[:, 0:16], F.Copy, scale=T.LOF[:, k + 4:k + 5]).then_inc(s.zls, 1)
-        xi()
-        P.wait_ge(s.zls, 4)
+        xi(V.tensor_copy(T.LOB[0:16, :], T.LO[0:16, :]))
+        P.matmul(T.psA[:, 0:128], T.BDb[0:16, :], T.LOB[0:16, :], True, True).then_inc(s.pa, 1)
+        P.matmul(T.psB[:, 0:128], T.BDo[0:16, :], T.LOB[0:16, :], True, True).then_inc(s.pb, 1)
+        V.wait_ge(s.po, 1)
+        vi(ts(T.hq[:, :], T.psO[:, 0:16], 0.0625, A.mult, -0.46875, A.add))
+        vw()
         vi(V.tensor_copy(T.off[:, :], T.hq[:, :]))
-        pei(P.matmul(T.psA[:, 0:128], T.BD[:, :], T.ZL[:, :], True, True))
-        vi(ts(T.E[:, :], T.psA[:, 0:128], T.rf[:, 0:1], A.is_equal))
+        V.wait_ge(s.pa, 1)
+        vi(ts(T.Eb[:, :], T.psA[:, 0:128], T.rf[:, 0:1], A.is_equal))
         vw()
         V.wait_ge(s.ldb, 128)
-        xi(V.tensor_tensor(T.XF[:, :], T.W16[:, :].indirect(T.off[:, 0:8]), T.E[:, :], A.mult))
-        pei(P.matmul(T.psF[:, 0:8], T.XF[:, :], T.eq8[:, :], True, True))
-        V.tensor_copy(T.b4s[:, :], T.psF[:, 0:8]).then_inc(s.dr, 1)
+        xi(V.tensor_tensor(T.XFb[:, :], T.W16[:, :].indirect(T.off[:, 0:8]), T.Eb[:, :], A.mult))
+        V.wait_ge(s.pb, 1)
+        vi(ts(T.Eo[:, :], T.psB[:, 0:128], T.rf[:, 0:1], A.is_equal))
+        pei(P.matmul(T.psF[:, 0:8], T.XFb[:, :], T.eq8[:, :], True, True))
+        V.tensor_copy(T.b4b[:, :], T.psF[:, 0:8]).then_inc(s.dr, 1)
         g.wait_ge(s.dr, 1)
         send(*sends[0])
-        vi(V.tensor_copy(T.SGF[:, :], T.SG[:, :]))
         vw()
-    else:
-        V.wait_ge(arrsem["b"], arrive["b"])
-    if f >= 4:
+        xi(V.tensor_tensor(T.XFo[:, :], T.W16[:, :].indirect(T.off[:, 8:16]), T.Eo[:, :], A.mult))
+        pei(P.matmul(T.psG[:, 0:8], T.XFo[:, :], T.eq8[:, :], True, True))
+        V.tensor_copy(T.b4o[:, :], T.psG[:, 0:8]).then_inc(s.do, 1)
+        g.wait_ge(s.do, 1)
+        send(*sends[1])
+        V.wait_ge(s.lsg, 128)
+        V.tensor_copy(T.offy[:, :], T.SG[:, :]).then_inc(s.oy, 1)
+    elif f == 4:
+        for q in (V, C):
+            q.wait_ge(s.arrb, arrive["b"])
+        C.wait_ge(s.cst, 1)
         for k in range(8):
-            cols, src = (T.Z[:, 8 * k:8 * k + 8], T.SGF) if f == 5 else (T.Z[:, k::8], T.b4)
-            vi(ts(cols, src[:, 0:8], T.eq8[:, k:k + 1], A.mult))
+            vi(V.tensor_copy(T.L4[0:64, 16 * k:16 * k + 16:2], T.b4[0:64, :]))
+            C.activation(T.L4[64:128, 16 * k + 1:16 * k + 16:2], T.b4[64:128, :], F.Copy).then_inc(s.l4, 1)
         xi()
+        P.wait_ge(s.l4, 8)
+        pei(P.matmul(T.psG[:, 0:64], T.L4[:, :], T.R4[:, :], True, True))
+        V.tensor_copy(T.offy[:, :], T.psG[:, 0:64]).then_inc(s.oy, 1)
     else:
-        vi(ts(T.hq[:, :], T.b4[:, :], 0.0625, A.mult, -0.46875, A.add))
-        vi(ts(T.t1[:, :], T.b4[:, :], 512.0, A.mult))
+        V.wait_ge(s.arrb, arrive["b" if f % 2 == 0 else "o"])
+        vi(ts(T.hq[:, 0:8], T.b4[:, :], 0.0625, A.mult, -0.46875, A.add))
+        vi(ts(T.u1[:, :], T.b4[:, :], 512.0, A.mult))
         vw()
-        vi(ts(T.t2[:, :], T.hq[:, :], -8191.0, A.mult))
+        vi(ts(T.u2[:, :], T.hq[:, 0:8], -8191.0, A.mult))
         vw()
-        vi(V.tensor_tensor(T.t3[:, :], T.t1[:, :], T.t2[:, :], A.add))
+        vi(V.tensor_tensor(T.u3[:, :], T.u1[:, :], T.u2[:, :], A.add))
         vw()
-        vi(V.tensor_copy(T.off[:, :], T.t3[:, :]))
+        vi(V.tensor_copy(T.off[:, 0:8], T.u3[:, :]))
         vw()
         for m in maps:
             w, k = place[m]
-            for mm in order:
+            for mm in ORDER[f]:
                 if place[mm][0] == w:
                     V.wait_ge(s["win%d" % mm], 128)
             xi(V.tensor_copy(T.X[:, :], T["W" + w][:, :].indirect(T.off[:, 0:8])))
             if m != maps[-1]:
                 pei(P.matmul(T.psA[:, 0:8], T.X[:, :], T["BP%d" % k][:, :], True, True))
-                vi(ts(T.off[:, :], T.psA[:, 0:8], 256.0, A.add))
+                vi(ts(T.off[:, 0:8], T.psA[:, 0:8], 256.0, A.add))
                 vw()
             else:
-                pei(P.matmul(T.psF[:, 0:64], T.X[:, :], T.BV[:, :], True, True))
-                xi(V.tensor_tensor(T.Z[:, :], T.psF[:, 0:64], T.MK[:, :], A.mult))
-    pei(P.matmul(T.psG[:, 0:64], T.R[:, :], T.Z[:, :], True, True))
-    ts(T.offy[:, :], T.psG[:, 0:64], 0.0 if f >= 4 else 4096.0, A.add).then_inc(s.oy, 1)
+                P.matmul(T.psF[:, 0:64], T.L0[:, :], T.X[:, 0:64], True, False)
+                pei(P.matmul(T.psF[:, 0:64], T.L1[:, :], T.X[:, 64:128], False, True))
+        ts(T.offy[:, :], T.psF[:, 0:64], 4096.0, A.add).then_inc(s.oy, 1)
 
     for q in (V, C):
         q.wait_ge(s.oy, 1)
-        q.wait_ge(s.tabl, 16 * NT)
+        q.wait_ge(s.tabl, 16 * len(LOAD[f]))
     V.tensor_copy(T.ya[:, :], T.tabs[:, :].indirect(T.offy[:, 0:32])).then_inc(s.yv, 1)
     C.wait_ge(s.cst, 1)
     C.activation(T.yb[:, :], T.tabs[:, :].indirect(T.offy[:, 32:64]), F.Identity, bias=T.nz[:, 0:1]).then_inc(s.ys, 1)

from concourse.bass import DstId, RemoteDMATransfer
from concourse.mybir import AluOpType as A, ActivationFunctionType as F

S = 8192
SCRATCH = {n: ("sbuf", [128, w], d) for d, lst in {
    "bfloat16": [("tabs", S), ("WA", S), ("WB", S), ("WC", S), ("zt", 1024), ("D", 128), ("X", 128), ("LOB", 128), ("BDb", 128),
                 ("BDo", 128), ("BP0", 8), ("BP1", 8), ("L0", 128), ("L1", 128), ("t0", 128), ("t1", 128), ("tx", 128), ("n8", 8),
                 ("lin", 64), ("ya", 512), ("yb", 512)],
    "float32": [("XFb", 128), ("Eb", 128), ("XFo", 128), ("Eo", 128), ("TF", 128), ("L4", 128), ("R4", 64), ("cg", 128),
                ("I16", 16), ("rf", 4), ("gf", 4), ("w1", 16), ("nz", 4), ("eq8", 8), ("b4b", 8), ("b4o", 8), ("b4", 8), ("u1", 8),
                ("u2", 8), ("u3", 8)],
    "int32": [("W16", 512), ("V2", 128), ("I2", 128), ("pi", 4), ("rg", 8), ("TT", 128), ("LO", 128), ("hq", 16), ("SG", 64)],
    "uint16": [("off", 16), ("offy", 64)]}.items() for n, w in lst}
SCRATCH.update({n: ("psum", [128, 512], "float32") for n in ("psA", "psB", "psF", "psG", "psO")})
SCRATCH.update({"land%d" % k: ("dram", [128, 128], "bfloat16") for k in (1, 2, 3, 4)})
SCRATCH["b4d"] = ("dram", [128, 8], "float32")
SEMAPHORES = ["v", "iot", "ipi", "ldb", "dr", "do", "sent", "tabl", "zz", "zA", "zB", "zC", "zAs", "zBs", "zCs", "zAg", "zBg",
              "zCg", "trg", "arr1", "arr2", "arr3", "arr4", "arrb", "arrc", "win1", "win2", "win3", "win4", "x", "pe", "po", "pa",
              "pb", "cst", "oy", "yv", "ys", "st", "lds", "lsg", "l4"]
TILES = {"t0": ([[0, 8], [1, 16]], 0), "t1": ([[0, 8], [1, 16]], -1), "n8": ([[1, 8]], 0), "lin": ([[1, 64]], 0),
         "I16": ([[1, 16]], 0), "cg": ([[1, 8], [0, 16]], 0)}
LOAD = {0: [(8192, "")], 1: [(3072, ""), (3072, "t"), (2048, "w")], 2: [(3072, ""), (3072, "t"), (2048, "w")],
        3: [(2048, ""), (2048, "t"), (4096, "s")], 4: [(2048, ""), (6144, "s")], 5: [(3072, ""), (5120, "s")]}
ORDER = {0: [2, 4, 3, 1], 1: [3, 2, 4], 2: [4, 3], 3: [4]}
FILLS = {0: [("V", "A", 0, S), ("V", "B", 0, 4096), ("g", "B", 4096, S), ("C", "C", 0, S)],
         1: [("V", "A", 0, 1024), ("V", "A", 1024, S), ("V", "B", 0, 1024), ("C", "B", 1024, 6144), ("t", "B", 6144, 6400),
             ("g", "B", 6400, S)],
         3: [("V", "A", 0, 1024), ("V", "A", 1024, 4096), ("C", "A", 4096, 7168), ("t", "A", 7168, 7424), ("g", "A", 7424, S)]}
FILLS[2] = FILLS[1]


def pick(mask, n):
    bits = [b for b in range(16) if mask >> b & 1][:8]
    n = min(n, len(bits))
    return sum(1 << b for b in bits[::len(bits) // n][:n])


def plan(T, topo):
    c = T.cores

    def chip(rank):
        own = c[rank]
        return [k for k in range(512) if topo.host(k) == topo.host(own) and topo.chip(k) == topo.chip(own) and k != own]

    def ports(rank, target):
        return sorted([k for k in chip(rank) if topo.may_write(k, c[target])], key=lambda k: (topo.die(k) != topo.die(c[rank]), k))

    p4, p2 = ports(2, 1)[0], ports(2, 1)[-1]
    p5, p3 = ports(3, 0)[0], ports(3, 0)[1]
    p1 = ports(1, 0)[0]
    p6 = [k for k in chip(3) if k not in ports(3, 0) and topo.may_write(k, c[1]) and topo.die(k) == topo.die(c[3])][0]
    return {
        c[5]: [("t1", [c[3]], 8), ("b", [p5], 8), ("o", [p6], 8)],
        p5: [("t1", [c[0]], 8), ("b", [c[0]], 8), ("b", [c[2]], 8), ("b", [c[4]], 8)],
        p6: [("n8", [c[1]], 8), ("o", [c[1]], 8), ("o", [c[3]], 8)],
        c[4]: [("t0", [c[2]], 8), (4, [p4, c[2]], 8)],
        p4: [("t0", [c[0]], 8), (4, [c[0]], 8), (4, [c[1]], 8), (4, [c[3]], 8)],
        c[3]: [("t0", [c[1]], 8), (3, [p3, c[1]], 8)],
        p3: [("t1", [c[2]], 4), (3, [c[0]], 4), (3, [c[2]], 4)],
        c[2]: [("lin", [c[4]], 8), (2, [p2, c[0]], 8)], p2: [("t1", [c[1]], 4), (2, [c[1]], 4)],
        c[1]: [("t0", [c[3]], 8), (1, [p1], 8)], p1: [("n8", [c[0]], 4), (1, [c[0]], 4)],
    }


def rank_program(g, core, T, topo):
    f = T.rank_of(core)
    calls = plan(T, topo)
    if core not in calls and f is None:
        return
    s = T.sem
    mine = calls.get(core, [])
    comes = [(piece, n) for lst in calls.values() for piece, dsts, n in lst if core in dsts]
    arrive = dict(comes)
    nconst = sum(n for piece, n in comes if piece in TILES)
    arrsem = {1: s.arr1, 2: s.arr2, 3: s.arr3, 4: s.arr4, "b": s.arrb, "o": s.arrb}
    nsent = sum(n for _, _, n in mine)
    niota = [0]

    def width(name):
        n = 1
        for _, k in TILES[name][0]:
            n *= k
        return n

    def send(piece, dsts, n):
        if piece in TILES:
            src, dst = T.tx[:, 0:width(piece)], T[piece][:, :]
        elif piece in ("b", "o"):
            src = T["b4" + piece][:, :] if f == 5 else T.b4d[:, :]
            dst = T.b4d[:, :] if f == 5 else T.b4[:, :]
        else:
            src = T.D[:, :] if f is not None else T["land%d" % piece][:, :]
            dst = T["land%d" % piece][:, :]
        mask = 0xFFFF
        for d in dsts:
            mask &= topo.mask(core, d)
        ids = [topo.addr(d, core) for d in dsts]
        g.remote_dma_fused([RemoteDMATransfer(dst_ids=[DstId(rid=r, pnc=p) for r, p in ids], dma_engine_mask=pick(mask, n),
                                              remote_sem=s.arrc if piece in TILES else arrsem[piece],
                                              srcs=[src], dsts=[dst] * len(dsts), alu_op=0)], local_sem=s.sent)

    def iota(name, out):
        pattern, base = TILES[name]
        g.iota(out, pattern, base, 0, allow_small_or_imprecise_dtypes=True).then_inc(s.iot, 1)
        niota[0] += 1

    if f is None:
        for k, c in enumerate(mine):
            if c[0] in TILES:
                iota(c[0], T.tx[:, 0:width(c[0])])
                g.wait_ge(s.iot, 1)
            elif k == 0 or mine[k - 1][0] in TILES:
                g.wait_ge(arrsem[c[0]], arrive[c[0]])
            send(*c)
        g.wait_ge(s.sent, nsent)
        return

    V, Q, C, P = g.vector, g.sync, g.scalar, g.tensor
    cnt = {"v": 0, "x": 0, "pe": 0}

    def vi(ins):
        cnt["v"] += 1
        return ins.then_inc(s.v, 1)

    def vw():
        V.wait_ge(s.v, cnt["v"])

    def xi(ins=None):
        cnt["x"] += 1
        if ins is None:
            vw()
            V.sem_inc(s.x, 1)
        else:
            ins.then_inc(s.x, 1)
        P.wait_ge(s.x, cnt["x"])

    def pei(ins):
        cnt["pe"] += 1
        ins.then_inc(s.pe, 1)
        V.wait_ge(s.pe, cnt["pe"])

    def ts(out, in0, s1, op0, s2=None, op1=None):
        if op1 is None:
            return V.tensor_scalar(out=out, in0=in0, scalar1=s1, scalar2=None, op0=op0)
        return V.tensor_scalar(out=out, in0=in0, scalar1=s1, scalar2=s2, op0=op0, op1=op1)

    if f == 5:
        Q.dma_start(T.TT[8:16, :], T.st[:, :]).then_inc(s.lds, 16)
        for c in range(8):
            (C, Q)[c % 2].dma_start(T.TT[c:c + 1, :], T.st[c // 4::2, 16 * (c % 4):16 * (c % 4) + 16]).then_inc(s.lds, 16)
        for k in range(8):
            (C, Q)[k % 2].dma_start(T.W16[16 * k:16 * k + 16, :], T.bp[:, :]).then_inc(s.ldb, 16)
        for k in range(8):
            C.dma_start(T.SG[16 * k:16 * k + 16, :], T.st[:, :]).then_inc(s.lsg, 16)
    elif f >= 1:
        Q.dma_start(T.V2[0:64, :], T.bp[:, :]).then_inc(s.ldb, 16)
        C.dma_start(T.V2[64:128, :], T.bp[:, :]).then_inc(s.ldb, 16)
    at = [0]

    def table(when):
        for w, t in LOAD[f]:
            if t == when:
                if t == "t":
                    Q.wait_ge(s.trg, 1)
                if t == "s":
                    Q.wait_ge(s.sent, nsent)
                Q.dma_start(T.tabs[:, at[0]:at[0] + w], T.tab[:, at[0]:at[0] + w]).then_inc(s.tabl, 16)
                at[0] += w

    for when in ("", "t", "s"):
        table(when)

    g.iota(T.pi[:, 0:1], [[1, 1]], 0, 1).then_inc(s.ipi, 1)
    need = [n for n in {3: ["t0", "t1"], 4: ["lin"], 5: ["n8", "I16", "cg"]}.get(f, ["t0", "t1", "n8"]) if n not in arrive]
    ahead = [c for c in mine if c[0] in TILES]
    if f == 5:
        for n in need:
            iota(n, T[n][:, :])
    for c in ahead:
        iota(c[0], T.tx[:, 0:width(c[0])])
        g.wait_ge(s.iot, niota[0])
        send(*c)
    if f != 5:
        for n in need:
            iota(n, T[n][:, :])
    sends = [c for c in mine if c[0] not in TILES]

    maps = list(range(4, f, -1))
    place = {0: {4: ("A", 0), 2: ("A", 1), 3: ("B", 0), 1: ("C", 0)}, 1: {4: ("A", 1), 2: ("A", 0), 3: ("B", 0)},
             2: {4: ("A", 0), 3: ("B", 0)}, 3: {4: ("A", 0)}}.get(f, {})

    def numbers():
        V.wait_ge(s.ipi, 1)
        vi(ts(T.rg[:, 0:1], T.pi[:, 0:1], 63 if f == 4 else 15, A.bitwise_and))
        vi(ts(T.rg[:, 4:5], T.pi[:, 0:1], 4, A.logical_shift_right))
        vw()
        vi(V.tensor_copy(T.rf[:, 0:1], T.rg[:, 0:1]))
        vi(V.tensor_copy(T.gf[:, 0:1], T.rg[:, 4:5]))
        if f == 5:
            vi(V.tensor_copy(T.gf[:, 2:3], T.pi[:, 0:1]))
            vi(ts(T.gf[:, 3:4], T.pi[:, 0:1], -8.0, A.add))
        else:
            vi(ts(T.gf[:, 1:2], T.rg[:, 4:5], 2.0, A.mult))
        vi(V.memset(T.nz[:, :], -0.0))

    def constants():
        vw()
        V.wait_ge(s.iot, niota[0])
        if nconst:
            V.wait_ge(s.arrc, nconst)
        r, gg = T.rf[:, 0:1], T.gf[:, 0:1]
        if f == 5:
            vi(ts(T.BDb[0:16, :], T.cg[0:16, :], T.gf[0:16, 3:4], A.is_equal))
            vi(ts(T.BDo[0:16, :], T.cg[0:16, :], T.gf[0:16, 2:3], A.is_equal))
            vi(ts(T.eq8[:, :], T.n8[:, :], gg, A.is_equal))
            vi(ts(T.I16[0:16, :], T.I16[0:16, :], T.gf[0:16, 2:3], A.is_equal))
        elif f == 4:
            vi(ts(T.R4[:, :], T.lin[:, :], r, A.is_equal))
            vi(V.memset(T.L4[:, :], 0.0))
        else:
            slots = sorted({place[m][1] for m in maps[:-1]})
            for k in slots:
                vi(ts(T.w1[:, 4 * k:4 * k + 1], r, float(2 * k), A.is_equal, 512.0, A.mult))
                vi(ts(T.w1[:, 4 * k + 1:4 * k + 2], r, float(2 * k + 1), A.is_equal))
            vi(ts(T.w1[:, 8:9], r, 0.0, A.is_equal))
            vi(ts(T.w1[:, 9:10], r, 1.0, A.is_equal, 16.0, A.mult))
            vw()
            for k in slots + [2]:
                vi(V.tensor_tensor(T.w1[:, 4 * k + 2:4 * k + 3], T.w1[:, 4 * k:4 * k + 1], T.w1[:, 4 * k + 1:4 * k + 2], A.add))
            vw()
            for k in slots:
                vi(ts(T["BP%d" % k][:, :], T.n8[:, :], gg, A.is_equal, T.w1[:, 4 * k + 2:4 * k + 3], A.mult))
            for e in (0, 1):
                vi(ts(T["L%d" % e][:, :], T["t%d" % e][:, :], T.gf[:, 1:2], A.is_equal, T.w1[:, 10:11], A.mult))
        vw()
        V.sem_inc(s.cst, 1)

    fills = FILLS.get(f, [])
    zeroed = {"A": {}, "B": {}, "C": {}}

    def fill(k, w, lo, hi):
        step = 1024 if k == "C" else hi - lo
        for a in range(lo, hi, step):
            out = T["W" + w][:, a:a + step]
            if k == "V":
                sem, ins = "z" + w, V.memset(out, 0.0)
            elif k == "C":
                sem, ins = "z" + w + "s", C.activation(out, T.zt[:, :], F.Copy)
            else:
                sem = "trg" if k == "t" else "z" + w + "g"
                ins = g.iota(out, [[0, step]], 0, 0, allow_small_or_imprecise_dtypes=True)
            ins.then_inc(s[sem], 1)
            zeroed[w][sem] = zeroed[w].get(sem, 0) + 1

    if fills:
        V.memset(T.zt[:, :], 0.0).then_inc(s.zz, 1)
        C.wait_ge(s.zz, 1)
    numbers()
    for z in fills[:1]:
        fill(*z)
    if 1 <= f <= 4:
        V.wait_ge(s.ldb, 32)
        vi(ts(T.I2[0:64, :], T.V2[0:64, :], 15, A.bitwise_and))
        vi(ts(T.I2[64:128, :], T.V2[64:128, :], 0.0625, A.mult, -256.46875, A.add))
        vw()
        V.tensor_copy(T.D[:, :], T.I2[:, :]).then_inc(s.dr, 1)
        g.wait_ge(s.dr, 1)
        send(*sends[0])
    for z in fills[1:]:
        fill(*z)
    constants()

    for m in ORDER.get(f, []):
        w, k = place[m]
        for q, half in ((Q, range(0, 4)), (C, range(4, 8))) if f else ((Q, range(8)),):
            q.wait_ge(arrsem[m], arrive[m])
            for z in zeroed[w].items():
                q.wait_ge(s[z[0]], z[1])
            for grp in half:
                lo = 16 * grp + 2 * k
                q.dma_start(T["W" + w][lo:lo + 2, :], T["land%d" % m][:, :]).then_inc(s["win%d" % m], 16)
    table("w")

    P.wait_ge(s.cst, 1)
    if f == 5:
        V.wait_ge(s.lds, 144)
        xi(V.tensor_copy(T.TF[0:16, :], T.TT[0:16, :]))
        P.matmul(T.psO[:, 0:16], T.TF[0:16, :], T.I16[0:16, :], True, True).then_inc(s.po, 1)
        vi(ts(T.LO[0:16, :], T.TT[0:16, :], 15, A.bitwise_and))
        vw()
        xi(V.tensor_copy(T.LOB[0:16, :], T.LO[0:16, :]))
        P.matmul(T.psA[:, 0:128], T.BDb[0:16, :], T.LOB[0:16, :], True, True).then_inc(s.pa, 1)
        P.matmul(T.psB[:, 0:128], T.BDo[0:16, :], T.LOB[0:16, :], True, True).then_inc(s.pb, 1)
        V.wait_ge(s.po, 1)
        vi(ts(T.hq[:, :], T.psO[:, 0:16], 0.0625, A.mult, -0.46875, A.add))
        vw()
        vi(V.tensor_copy(T.off[:, :], T.hq[:, :]))
        V.wait_ge(s.pa, 1)
        vi(ts(T.Eb[:, :], T.psA[:, 0:128], T.rf[:, 0:1], A.is_equal))
        vw()
        V.wait_ge(s.ldb, 128)
        xi(V.tensor_tensor(T.XFb[:, :], T.W16[:, :].indirect(T.off[:, 0:8]), T.Eb[:, :], A.mult))
        V.wait_ge(s.pb, 1)
        vi(ts(T.Eo[:, :], T.psB[:, 0:128], T.rf[:, 0:1], A.is_equal))
        pei(P.matmul(T.psF[:, 0:8], T.XFb[:, :], T.eq8[:, :], True, True))
        V.tensor_copy(T.b4b[:, :], T.psF[:, 0:8]).then_inc(s.dr, 1)
        g.wait_ge(s.dr, 1)
        send(*sends[0])
        vw()
        xi(V.tensor_tensor(T.XFo[:, :], T.W16[:, :].indirect(T.off[:, 8:16]), T.Eo[:, :], A.mult))
        pei(P.matmul(T.psG[:, 0:8], T.XFo[:, :], T.eq8[:, :], True, True))
        V.tensor_copy(T.b4o[:, :], T.psG[:, 0:8]).then_inc(s.do, 1)
        g.wait_ge(s.do, 1)
        send(*sends[1])
        V.wait_ge(s.lsg, 128)
        V.tensor_copy(T.offy[:, :], T.SG[:, :]).then_inc(s.oy, 1)
    elif f == 4:
        for q in (V, C):
            q.wait_ge(s.arrb, arrive["b"])
        C.wait_ge(s.cst, 1)
        for k in range(8):
            vi(V.tensor_copy(T.L4[0:64, 16 * k:16 * k + 16:2], T.b4[0:64, :]))
            C.activation(T.L4[64:128, 16 * k + 1:16 * k + 16:2], T.b4[64:128, :], F.Copy).then_inc(s.l4, 1)
        xi()
        P.wait_ge(s.l4, 8)
        pei(P.matmul(T.psG[:, 0:64], T.L4[:, :], T.R4[:, :], True, True))
        V.tensor_copy(T.offy[:, :], T.psG[:, 0:64]).then_inc(s.oy, 1)
    else:
        V.wait_ge(s.arrb, arrive["b" if f % 2 == 0 else "o"])
        vi(ts(T.hq[:, 0:8], T.b4[:, :], 0.0625, A.mult, -0.46875, A.add))
        vi(ts(T.u1[:, :], T.b4[:, :], 512.0, A.mult))
        vw()
        vi(ts(T.u2[:, :], T.hq[:, 0:8], -8191.0, A.mult))
        vw()
        vi(V.tensor_tensor(T.u3[:, :], T.u1[:, :], T.u2[:, :], A.add))
        vw()
        vi(V.tensor_copy(T.off[:, 0:8], T.u3[:, :]))
        vw()
        for m in maps:
            w, k = place[m]
            for mm in ORDER[f]:
                if place[mm][0] == w:
                    V.wait_ge(s["win%d" % mm], 128)
            xi(V.tensor_copy(T.X[:, :], T["W" + w][:, :].indirect(T.off[:, 0:8])))
            if m != maps[-1]:
                pei(P.matmul(T.psA[:, 0:8], T.X[:, :], T["BP%d" % k][:, :], True, True))
                vi(ts(T.off[:, 0:8], T.psA[:, 0:8], 256.0, A.add))
                vw()
            else:
                P.matmul(T.psF[:, 0:64], T.L0[:, :], T.X[:, 0:64], True, False)
                pei(P.matmul(T.psF[:, 0:64], T.L1[:, :], T.X[:, 64:128], False, True))
        ts(T.offy[:, :], T.psF[:, 0:64], 4096.0, A.add).then_inc(s.oy, 1)

    for q in (V, C):
        q.wait_ge(s.oy, 1)
        q.wait_ge(s.tabl, 16 * len(LOAD[f]))
    V.tensor_copy(T.ya[:, :], T.tabs[:, :].indirect(T.offy[:, 0:32])).then_inc(s.yv, 1)
    C.wait_ge(s.cst, 1)
    C.activation(T.yb[:, :], T.tabs[:, :].indirect(T.offy[:, 32:64]), F.Identity, bias=T.nz[:, 0:1]).then_inc(s.ys, 1)
    Q.wait_ge(s.yv, 1)
    Q.dma_start(T.y[:, 0:512], T.ya[:, :]).then_inc(s.st, 16)
    C.wait_ge(s.ys, 1)
    C.dma_start(T.y[:, 512:1024], T.yb[:, :]).then_inc(s.st, 16)
    Q.wait_ge(s.st, 32)
    if nsent:
        g.wait_ge(s.sent, nsent)
